import numpy as np
import ml_dtypes


def mxq(x, axis, fmt="e4m3"):
    dtype, down = {"e4m3": (ml_dtypes.float8_e4m3fn, 7), "e5m2": (ml_dtypes.float8_e5m2, 14)}[fmt]
    v = np.moveaxis(np.asarray(x, np.float32).astype(ml_dtypes.bfloat16).astype(np.float64), axis, -1)
    blocks = v.reshape(v.shape[:-1] + (-1, 32))
    amax = np.abs(blocks).max(-1, keepdims=True)
    byte = np.maximum(np.where(amax > 0, np.frexp(amax)[1] - 1 + 127, 0) - down, 1)
    scale = np.exp2(byte - 127.0)
    codes = (blocks / scale).astype(np.float32).astype(dtype).astype(np.float64)
    return np.moveaxis((codes * scale).reshape(v.shape), -1, axis)


WIDE = False


def mx_kscale(k):
    if not WIDE:
        return np.ones(k)
    levels = np.array([10, -10, 5, -5, 0])
    if k % 512:
        return np.exp2(np.random.permutation(np.resize(levels, k // 32))).repeat(32)
    a = np.empty((k // 512, 16))
    for p in range(k // 512):
        a[p, :8] = np.random.permutation(np.resize(levels, 8))
        for g in range(8):
            far = levels[np.abs(levels - a[p, g]) >= 10]
            a[p, g + 8] = far[np.random.randint(len(far))]
    return np.exp2(a.ravel()).repeat(32)


def f64(x):
    return np.asarray(x).astype(np.float64)


def striped(idx):
    return np.tile(idx.reshape(-1, 16).T, (8, 1)).astype(np.uint16)


def unstriped(offs):
    return offs[:16].T.reshape(-1).astype(np.int64)


def striped8(idx):
    return np.concatenate([x.reshape(-1, 16).T for x in idx]).astype(np.uint16)


def runs(offs, k):
    lists = np.stack([offs[16 * r : 16 * r + 16].T.reshape(-1) for r in range(8)]).astype(np.int64)
    return lists[np.arange(k) % 512 // 64]


def pack_weight(w):
    k, n = w.shape
    w = f64(np.asarray(w, np.float32).astype(ml_dtypes.bfloat16)).reshape(k // 32, 32, n)
    amax = np.abs(w).max(1)
    byte = np.clip(np.where(amax > 0, np.frexp(amax)[1] - 1 + 127 - 7, 1), 1, 254)
    scaled = (w * np.exp2(127.0 - byte)[:, None, :]).reshape(k, n).astype(np.float32)
    words = np.ascontiguousarray(scaled.reshape(k // 512, 128, 4, n).transpose(0, 1, 3, 2)).astype(ml_dtypes.float8_e4m3fn).view(np.uint8)
    return words, np.ascontiguousarray(byte.astype(np.uint8).reshape(k // 512, 16, n))


def unpack_weight(words, scales):
    g, p, n, _ = words.shape
    vals = np.ascontiguousarray(words).view(ml_dtypes.float8_e4m3fn).astype(np.float64) * np.repeat(np.exp2(scales.astype(np.float64) - 127.0), 8, axis=1)[..., None]
    return vals.transpose(0, 1, 3, 2).reshape(g * 512, n)


E2M1 = np.array([0.0, 0.5, 1.0, 1.5, 2.0, 3.0, 4.0, 6.0, -0.0, -0.5, -1.0, -1.5, -2.0, -3.0, -4.0, -6.0])


def pack_fp4(w):
    k, n = w.shape
    w = f64(np.asarray(w, np.float32).astype(ml_dtypes.bfloat16)).reshape(k // 32, 32, n)
    amax = np.abs(w).max(1)
    mant, ex = np.frexp(amax / 6.0)
    byte = np.clip(np.where(amax > 0, np.where(mant > 0.5, ex, ex - 1) + 127, 1), 1, 254)
    scaled = (w * np.exp2(127.0 - byte)[:, None, :]).reshape(k, n).astype(np.float32)
    c = np.ascontiguousarray(scaled.reshape(k // 512, 128, 4, n).transpose(0, 1, 3, 2)).astype(ml_dtypes.float4_e2m1fn).view(np.uint8) & 0xF
    words = (c[..., 0::2] | (c[..., 1::2] << 4)).reshape(k // 512, 128, 2 * n)
    return np.ascontiguousarray(words), np.ascontiguousarray(byte.astype(np.uint8).reshape(k // 512, 16, n))


def unpack_fp4(words, scales):
    g, _, n = scales.shape
    words = np.ascontiguousarray(words).reshape(g, 128, n, 2)
    nib = np.empty((g, 128, n, 4), np.uint8)
    nib[..., 0::2] = words & 0xF
    nib[..., 1::2] = words >> 4
    vals = E2M1[nib] * np.repeat(np.exp2(scales.astype(np.float64) - 127.0), 8, axis=1)[..., None]
    return vals.transpose(0, 1, 3, 2).reshape(g * 512, n)


def planes(y):
    n, m = y.shape
    v = y.astype(np.float32).astype(ml_dtypes.bfloat16).astype(np.float64).reshape(n // 32, 32, m)
    top = np.abs(v).max(1)
    byte = np.clip(np.where(top > 0, np.frexp(top)[1] - 1 + 127 - 7, 1), 1, 254)
    codes = (v * np.exp2(127.0 - byte)[:, None, :]).reshape(n, m).astype(np.float32).astype(ml_dtypes.float8_e4m3fn).view(np.uint8)
    words = codes.reshape(n // 512, 128, 4, m).transpose(0, 1, 3, 2)
    return np.ascontiguousarray(words), np.ascontiguousarray(byte.astype(np.uint8).reshape(n // 512, 16, m))


K, T, S, H, G = 512, 1024, 256, 512, 2048


def setup_inputs():
    n = np.random.standard_normal
    s = mx_kscale(K)[:, None]
    packed_xT = pack_weight(n((K, T)) * s)
    packed_w1 = pack_fp4(n((K, H)) / np.sqrt(K) / s)
    packed_w2 = pack_fp4(n((K, H)) / np.sqrt(K) / s)
    packed_dT = pack_weight(n((K, G)) / s)
    return {
        "x_words": packed_xT[0],
        "x_scales": packed_xT[1],
        "w1_words": packed_w1[0],
        "w1_scales": packed_w1[1],
        "w2_words": packed_w2[0],
        "w2_scales": packed_w2[1],
        "gs": (np.random.uniform(0.5, 1.5, (K, 1)) * s).astype(np.float32),
        "d_words": packed_dT[0],
        "d_scales": packed_dT[1],
        "offs": striped(np.random.permutation(T)[:S]),
        "two": striped(np.random.permutation(T)[:S]),
        "n1": striped8(np.stack([np.random.permutation(S) for _ in range(8)])),
        "n2": striped8(np.stack([np.random.permutation(S) for _ in range(8)])),
        "n3": striped8(np.stack([np.random.permutation(S) for _ in range(8)])),
        "k1": striped8(np.random.randint(0, G, (8, H))),
        "n4": striped(np.random.permutation(S)),
        "n5": striped(np.random.permutation(S)),
    }


def reference(x_words, x_scales, w1_words, w1_scales, w2_words, w2_scales, gs, d_words, d_scales, offs, two, n1, n2, n3, k1, n4, n5):
    d_k1 = unpack_weight(d_words, d_scales)[np.arange(K)[:, None], runs(k1, K)]
    x_two = unpack_weight(x_words, x_scales)[:, unstriped(two)]
    d = unpack_fp4(w2_words, w2_scales).T @ x_two
    xq = unpack_weight(x_words, x_scales)[:, unstriped(offs)]
    y = unpack_fp4(w1_words, w1_scales).T @ xq
    z = f64(gs) * (d * (y[np.arange(H)[:, None], runs(n1, H)] - y) + 0.5 * ((d[np.arange(H)[:, None], runs(n3, H)]) * (y[np.arange(H)[:, None], runs(n2, H)] - y)))
    h = 0.0625 * ((d_k1.T @ mxq(z, 0, "e4m3")))
    ex = np.exp(0.5 * h)
    out_0 = (2.0 * ex) / (ex + ex[:, unstriped(n4)] + ex[:, unstriped(n5)])
    return (out_0,) + planes(out_0)

@@ -1,0 +1,228 @@
+from contextlib import ExitStack
+
+import concourse.mybir as mybir
+
+K, T, S, H, G = 512, 1024, 256, 512, 2048
+FLOPS = 3 * 2 * K * H * S
+
+F32 = mybir.dt.float32
+BF16 = mybir.dt.bfloat16
+I32 = mybir.dt.int32
+U32 = mybir.dt.uint32
+U16 = mybir.dt.uint16
+U8 = mybir.dt.uint8
+FP8X4 = mybir.dt.float8_e4m3fn_x4
+FP4X4 = mybir.dt.float4_e2m1fn_x4
+ACT = mybir.ActivationFunctionType
+ALU = mybir.AluOpType
+
+P = 128
+PACK = 4
+WIN = 2 * S
+
+
+def tile_picked_twqflowbshare_none_po_kernel(
+    tc, x_words, x_scales, w1_words, w1_scales, w2_words, w2_scales, gs, d_words, d_scales,
+    offs, two, n1, n2, n3, k1, n4, n5, out_0, out_1, out_2,
+):
+    nc = tc.nc
+    with ExitStack() as ctx:
+        keep = ctx.enter_context(tc.tile_pool(name="keep", bufs=1))
+        psum = ctx.enter_context(tc.psum_pool(name="psum", bufs=1))
+
+        def sb(name, shape, dtype):
+            return keep.tile(shape, dtype, name=name, align_bytes=64)
+
+        def load_list(name, src):
+            tile = keep.tile(list(src.shape), U16, name=name)
+            nc.sync.dma_start(tile[:], src)
+            return tile
+
+        def load_scale_rows(queue, tile, scales):
+            for q in range(4):
+                queue.dma_start(tile[32 * q : 32 * q + 4, :].bitcast(I32), scales[0, 4 * q : 4 * q + 4, :].bitcast(I32))
+
+        x_scale_table = sb("x_scale_table", [P, T], U8)
+        w1_scale_raw = sb("w1_scale_raw", [P, H], U8)
+        w2_scale_raw = sb("w2_scale_raw", [P, H], U8)
+        d_scale_table = sb("d_scale_table", [P, G], U8)
+        nc.gpsimd.memset(x_scale_table[:].bitcast(I32), 0)
+        nc.gpsimd.memset(w1_scale_raw[:].bitcast(I32), 0)
+        nc.gpsimd.memset(w2_scale_raw[:].bitcast(I32), 0)
+        nc.vector.memset(d_scale_table[:].bitcast(I32), 0)
+
+        offs_sb = load_list("offs_sb", offs)
+        w1_raw = sb("w1_raw", [P, 2 * H], U8)
+        nc.sync.dma_start(w1_raw[:].bitcast(I32), w1_words[0].bitcast(I32))
+        load_scale_rows(nc.sync, x_scale_table, x_scales)
+        x_table = sb("x_table", [P, T], U32)
+        nc.sync.dma_start(x_table[:].bitcast(I32), x_words[0].rearrange("p n t -> p (n t)").bitcast(I32))
+        two_sb = load_list("two_sb", two)
+        load_scale_rows(nc.sync, w1_scale_raw, w1_scales)
+        w2_raw = sb("w2_raw", [P, 2 * H], U8)
+        nc.sync.dma_start(w2_raw[:].bitcast(I32), w2_words[0].bitcast(I32))
+        n1_sb = load_list("n1_sb", n1)
+        n2_sb = load_list("n2_sb", n2)
+        load_scale_rows(nc.sync, w2_scale_raw, w2_scales)
+        gs_sb = sb("gs_sb", [P, PACK], F32)
+        nc.sync.dma_start(gs_sb[:], gs.rearrange("(p t) o -> p (t o)", t=PACK))
+        n3_sb = load_list("n3_sb", n3)
+        k1_sb = load_list("k1_sb", k1)
+        for e in range(2):
+            nc.sync.dma_start(d_scale_table[e:P:16, :].bitcast(I32), d_scales[0, e:16:2, :].bitcast(I32))
+        d_table = sb("d_table", [P, G], U32)
+        nc.sync.dma_start(d_table[:].bitcast(I32), d_words[0].rearrange("p n t -> p (n t)").bitcast(I32))
+        n4_sb = load_list("n4_sb", n4)
+        n5_sb = load_list("n5_sb", n5)
+
+        y_win = [sb(f"y_win{t}", [P, WIN], F32) for t in range(PACK)]
+        d_win = [sb(f"d_win{t}", [P, WIN], F32) for t in range(PACK)]
+        e_win = [sb(f"e_win{t}", [P, WIN], F32) for t in range(PACK)]
+        for t in range(PACK):
+            nc.vector.memset(y_win[t][:, S:], 0.0)
+            nc.gpsimd.memset(e_win[t][:, S:], 0.0)
+
+        def deal_words(name, w_raw):
+            dealt = sb(name, [P, 2 * H], U8)
+            nc.vector.tensor_copy(
+                dealt[:].rearrange("p (t m b) -> p t m b", t=PACK, b=2),
+                w_raw[:].rearrange("p (m t b) -> p t m b", t=PACK, b=2),
+            )
+            return dealt
+
+        def deal(name, raw, dtype):
+            dealt = sb(name, [P, H], dtype)
+            nc.vector.tensor_copy(
+                dealt[:].rearrange("p (t m) -> p t m", t=PACK),
+                raw[:].rearrange("p (m t) -> p t m", t=PACK),
+            )
+            return dealt
+
+        def pick(name, table, offsets, count, dtype):
+            picked = sb(name, [P, count], dtype)
+            nc.vector.tensor_copy(picked[:], table[:].indirect(offsets[:]))
+            return picked
+
+        def project(name, w_dealt, w_scale_dealt, words, scales):
+            banks = []
+            for t in range(PACK):
+                bank = psum.tile([P, S], F32, name=f"{name}_bank{t}", tag=f"{name}{t}")
+                nc.tensor.matmul_mx(
+                    out=bank[:],
+                    lhsT=w_dealt[:, 2 * P * t : 2 * P * (t + 1)].bitcast(FP4X4),
+                    lhsT_scale=w_scale_dealt[:, P * t : P * (t + 1)],
+                    rhs=words[:].bitcast(FP8X4),
+                    rhs_scale=scales[:],
+                    start=True,
+                    stop=True,
+                )
+                banks.append(bank)
+            return banks
+
+        w1_dealt = deal_words("w1_dealt", w1_raw)
+        xq_scales = pick("xq_scales", x_scale_table, offs_sb, S, U8)
+        xq_words = pick("xq_words", x_table, offs_sb, S, U32)
+        w1_scale_dealt = deal("w1_scale_dealt", w1_scale_raw, U8)
+        y_banks = project("y", w1_dealt, w1_scale_dealt, xq_words, xq_scales)
+        x2_scales = pick("x2_scales", x_scale_table, two_sb, S, U8)
+        x2_words = pick("x2_words", x_table, two_sb, S, U32)
+        w2_dealt = deal_words("w2_dealt", w2_raw)
+        w2_scale_dealt = deal("w2_scale_dealt", w2_scale_raw, U8)
+        d_banks = project("d", w2_dealt, w2_scale_dealt, x2_words, x2_scales)
+
+        code_picked = sb("code_picked", [P, H], U32)
+        code_scale_picked = sb("code_scale_picked", [P, H], U8)
+        code_dealt = sb("code_dealt", [P, H], U32)
+        code_scale_dealt = sb("code_scale_dealt", [P, H], U8)
+        nc.vector.tensor_copy(code_scale_picked[:], d_scale_table[:].indirect(k1_sb[:]))
+        nc.vector.tensor_copy(
+            code_scale_dealt[:].rearrange("p (t m) -> p t m", t=PACK),
+            code_scale_picked[:].rearrange("p (m t) -> p t m", t=PACK),
+        )
+        for e in range(2):
+            nc.sync.dma_start(code_scale_dealt[2 + e : P : 32, :].bitcast(I32), code_scale_dealt[16 + e : P : 32, :].bitcast(I32))
+        nc.vector.tensor_copy(code_picked[:], d_table[:].indirect(k1_sb[:]))
+        nc.vector.tensor_copy(
+            code_dealt[:].rearrange("p (t m) -> p t m", t=PACK),
+            code_picked[:].rearrange("p (m t) -> p t m", t=PACK),
+        )
+
+        y_n2 = sb("y_n2", [P, PACK, S], F32)
+        d_n3 = sb("d_n3", [P, PACK, S], F32)
+        diff1 = sb("diff1", [P, PACK, S], F32)
+        diff2 = sb("diff2", [P, PACK, S], F32)
+        term1 = sb("term1", [P, PACK, S], F32)
+        term2 = sb("term2", [P, PACK, S], F32)
+        for t in range(PACK):
+            y = y_win[t][:, :S]
+            dg = d_win[t][:, :S]
+            y_n1 = d_win[t][:, S:]
+            nc.scalar.activation(y, y_banks[t][:], ACT.Copy)
+            nc.scalar.activation(y_n1, y_win[t][:].indirect(n1_sb[:]), ACT.Copy)
+            nc.scalar.activation(y_n2[:, t, :], y_win[t][:].indirect(n2_sb[:]), ACT.Copy)
+            nc.scalar.activation(dg, d_banks[t][:], ACT.Copy, scale=gs_sb[:, t : t + 1])
+            nc.scalar.activation(d_n3[:, t, :], d_win[t][:].indirect(n3_sb[:]), ACT.Copy)
+            nc.vector.tensor_tensor(diff1[:, t, :], y_n1, y, ALU.subtract)
+            nc.vector.tensor_tensor(diff2[:, t, :], y_n2[:, t, :], y, ALU.subtract)
+            nc.vector.tensor_tensor(term1[:, t, :], diff1[:, t, :], dg, ALU.mult)
+            nc.vector.scalar_tensor_tensor(term2[:, t, :], d_n3[:, t, :], 0.5, diff2[:, t, :], ALU.mult, ALU.mult)
+
+        z_bf = sb("z_bf", [P, S, PACK], BF16)
+        nc.vector.tensor_tensor(
+            z_bf[:].rearrange("p (c i) t -> p c t i", i=4),
+            term1[:].rearrange("p t (c i) -> p c t i", i=4),
+            term2[:].rearrange("p t (c i) -> p c t i", i=4),
+            ALU.add,
+        )
+        z_words = sb("z_words", [P, S], U32)
+        z_scales = sb("z_scales", [P, S], U8)
+        nc.vector.quantize_mx(out=z_words[:].bitcast(FP8X4), scales=z_scales[:], in_=z_bf[:].rearrange("p j t -> p (j t)"))
+
+        h_banks = []
+        for t in range(PACK):
+            bank = psum.tile([P, S], F32, name=f"h_bank{t}", tag=f"y{t}")
+            nc.tensor.matmul_mx(
+                out=bank[:],
+                lhsT=code_dealt[:, P * t : P * (t + 1)].bitcast(FP8X4),
+                lhsT_scale=code_scale_dealt[:, P * t : P * (t + 1)],
+                rhs=z_words[:].bitcast(FP8X4),
+                rhs_scale=z_scales[:],
+                start=True,
+                stop=True,
+            )
+            h_banks.append(bank)
+
+        e_n4 = sb("e_n4", [P, PACK, S], F32)
+        e_n5 = sb("e_n5", [P, PACK, S], F32)
+        part = sb("part", [P, PACK, S], F32)
+        total = sb("total", [P, PACK, S], F32)
+        root = sb("root", [P, PACK, S], F32)
+        half = sb("half", [P, PACK, S], F32)
+        result = sb("result", [P, PACK, S], F32)
+        for t in range(PACK):
+            nc.scalar.activation(e_win[t][:, :S], h_banks[t][:], ACT.Exp, scale=0.03125)
+        for t in range(PACK):
+            nc.vector.tensor_copy(e_n5[:, t, :], e_win[t][:].indirect(n5_sb[:]))
+            nc.scalar.activation(e_n4[:, t, :], e_win[t][:].indirect(n4_sb[:]), ACT.Copy)
+            nc.vector.tensor_tensor(part[:, t, :], e_n5[:, t, :], e_win[t][:, :S], ALU.add)
+        for t in range(PACK):
+            nc.vector.tensor_tensor(total[:, t, :], part[:, t, :], e_n4[:, t, :], ALU.add)
+        out_rows = out_0.rearrange("(p t) j -> p t j", t=PACK)
+        for t in range(PACK):
+            nc.scalar.activation(root[:, t, :], total[:, t, :], ACT.Abs_reciprocal_sqrt, scale=0.5)
+            nc.vector.tensor_tensor(half[:, t, :], root[:, t, :], e_win[t][:, :S], ALU.mult)
+            nc.vector.tensor_tensor(result[:, t, :], half[:, t, :], root[:, t, :], ALU.mult)
+            nc.sync.dma_start(out_rows[:, t, :], result[:, t, :])
+
+        result_bf = sb("result_bf", [P, S, PACK], BF16)
+        nc.vector.tensor_copy(
+            result_bf[:].rearrange("p (c i) t -> p c t i", i=4),
+            result[:].rearrange("p t (c i) -> p c t i", i=4),
+        )
+        out_words = sb("out_words", [P, S], U32)
+        out_scales = sb("out_scales", [P, S], U8)
+        nc.vector.quantize_mx(out=out_words[:].bitcast(FP8X4), scales=out_scales[:], in_=result_bf[:].rearrange("p j t -> p (j t)"))
+        nc.sync.dma_start(out_1[0].rearrange("p n t -> p (n t)").bitcast(I32), out_words[:].bitcast(I32))
+        for q in range(4):
+            queue = nc.scalar if q % 2 == 0 else nc.sync
+            queue.dma_start(out_2[0, 4 * q : 4 * q + 4, :].bitcast(I32), out_scales[32 * q : 32 * q + 4, :].bitcast(I32))

@@ -40,16 +40,19 @@ def tile_picked_twqflowbshare_none_po_kernel(
 
         def load_scale_rows(queue, tile, scales):
             for q in range(4):
-                queue.dma_start(tile[32 * q : 32 * q + 4, :].bitcast(I32), scales[0, 4 * q : 4 * q + 4, :].bitcast(I32))
+                rows = scales[0, 4 * q : 4 * q + 4, :].bitcast(I32)
+                queue.dma_start(tile[32 * q : 32 * q + 32, :].bitcast(I32), rows.unsqueeze(0).broadcast_to([8, *rows.shape]))
 
         x_scale_table = sb("x_scale_table", [P, T], U8)
         w1_scale_raw = sb("w1_scale_raw", [P, H], U8)
-        w2_scale_raw = sb("w2_scale_raw", [P, H], U8)
+        w2_scale_raw = keep.tile([P, H], U8, name="w2_scale_raw", tag="stage", align_bytes=64)
         d_scale_table = sb("d_scale_table", [P, G], U8)
-        nc.gpsimd.memset(x_scale_table[:].bitcast(I32), 0)
-        nc.gpsimd.memset(w1_scale_raw[:].bitcast(I32), 0)
-        nc.gpsimd.memset(w2_scale_raw[:].bitcast(I32), 0)
-        nc.vector.memset(d_scale_table[:].bitcast(I32), 0)
+        nc.gpsimd.memset(d_scale_table[:].bitcast(I32), 0)
+
+        for e in range(2):
+            nc.gpsimd.dma_start(d_scale_table[e:P:16, :].bitcast(I32), d_scales[0, e:16:2, :].bitcast(I32))
+        gs_sb = sb("gs_sb", [P, PACK], F32)
+        nc.gpsimd.dma_start(gs_sb[:], gs.rearrange("(p t) o -> p (t o)", t=PACK))
 
         offs_sb = load_list("offs_sb", offs)
         w1_raw = sb("w1_raw", [P, 2 * H], U8)
@@ -64,29 +67,26 @@ def tile_picked_twqflowbshare_none_po_kernel(
         n1_sb = load_list("n1_sb", n1)
         n2_sb = load_list("n2_sb", n2)
         load_scale_rows(nc.sync, w2_scale_raw, w2_scales)
-        gs_sb = sb("gs_sb", [P, PACK], F32)
-        nc.sync.dma_start(gs_sb[:], gs.rearrange("(p t) o -> p (t o)", t=PACK))
-        n3_sb = load_list("n3_sb", n3)
         k1_sb = load_list("k1_sb", k1)
-        for e in range(2):
-            nc.sync.dma_start(d_scale_table[e:P:16, :].bitcast(I32), d_scales[0, e:16:2, :].bitcast(I32))
         d_table = sb("d_table", [P, G], U32)
         nc.sync.dma_start(d_table[:].bitcast(I32), d_words[0].rearrange("p n t -> p (n t)").bitcast(I32))
+        n3_sb = load_list("n3_sb", n3)
         n4_sb = load_list("n4_sb", n4)
         n5_sb = load_list("n5_sb", n5)
 
         y_win = [sb(f"y_win{t}", [P, WIN], F32) for t in range(PACK)]
         d_win = [sb(f"d_win{t}", [P, WIN], F32) for t in range(PACK)]
-        e_win = [sb(f"e_win{t}", [P, WIN], F32) for t in range(PACK)]
+        e_win = [sb(f"e_win{t}", [P, S + 16], F32) for t in range(PACK)]
         for t in range(PACK):
             nc.vector.memset(y_win[t][:, S:], 0.0)
-            nc.gpsimd.memset(e_win[t][:, S:], 0.0)
+            nc.scalar.activation(d_win[t][:, S:], y_win[t][:, S:], ACT.Copy)
+            nc.vector.memset(e_win[t][:, S:], 0.0)
 
         def deal_words(name, w_raw):
             dealt = sb(name, [P, 2 * H], U8)
             nc.vector.tensor_copy(
-                dealt[:].rearrange("p (t m b) -> p t m b", t=PACK, b=2),
-                w_raw[:].rearrange("p (m t b) -> p t m b", t=PACK, b=2),
+                dealt[:].bitcast(U16).rearrange("p (t m) -> p t m", t=PACK),
+                w_raw[:].bitcast(U16).rearrange("p (m t) -> p t m", t=PACK),
             )
             return dealt
 
@@ -130,8 +130,7 @@ def tile_picked_twqflowbshare_none_po_kernel(
         w2_scale_dealt = deal("w2_scale_dealt", w2_scale_raw, U8)
         d_banks = project("d", w2_dealt, w2_scale_dealt, x2_words, x2_scales)
 
-        code_picked = sb("code_picked", [P, H], U32)
-        code_scale_picked = sb("code_scale_picked", [P, H], U8)
+        code_scale_picked = keep.tile([P, H], U8, name="code_scale_picked", tag="stage", align_bytes=64)
         code_dealt = sb("code_dealt", [P, H], U32)
         code_scale_dealt = sb("code_scale_dealt", [P, H], U8)
         nc.vector.tensor_copy(code_scale_picked[:], d_scale_table[:].indirect(k1_sb[:]))
@@ -141,83 +140,89 @@ def tile_picked_twqflowbshare_none_po_kernel(
         )
         for e in range(2):
             nc.sync.dma_start(code_scale_dealt[2 + e : P : 32, :].bitcast(I32), code_scale_dealt[16 + e : P : 32, :].bitcast(I32))
+        code_picked = keep.tile([P, H], U32, name="code_picked", tag="stage", align_bytes=64)
         nc.vector.tensor_copy(code_picked[:], d_table[:].indirect(k1_sb[:]))
         nc.vector.tensor_copy(
             code_dealt[:].rearrange("p (t m) -> p t m", t=PACK),
             code_picked[:].rearrange("p (m t) -> p t m", t=PACK),
         )
 
-        y_n2 = sb("y_n2", [P, PACK, S], F32)
-        d_n3 = sb("d_n3", [P, PACK, S], F32)
-        diff1 = sb("diff1", [P, PACK, S], F32)
-        diff2 = sb("diff2", [P, PACK, S], F32)
+        y_near = [sb(f"y_near{t}", [P, 2, S], F32) for t in range(PACK)]
+        d_n3 = [sb(f"d_n3_{t}", [P, S], F32) for t in range(PACK)]
+        diff = keep.tile([P, PACK, 2, S], F32, name="diff", tag="stage", align_bytes=64)
         term1 = sb("term1", [P, PACK, S], F32)
         term2 = sb("term2", [P, PACK, S], F32)
+        halves = [slice(0, S // 2), slice(S // 2, S)]
         for t in range(PACK):
             y = y_win[t][:, :S]
             dg = d_win[t][:, :S]
-            y_n1 = d_win[t][:, S:]
             nc.scalar.activation(y, y_banks[t][:], ACT.Copy)
-            nc.scalar.activation(y_n1, y_win[t][:].indirect(n1_sb[:]), ACT.Copy)
-            nc.scalar.activation(y_n2[:, t, :], y_win[t][:].indirect(n2_sb[:]), ACT.Copy)
+            nc.scalar.activation(y_near[t][:, 0, :], y_win[t][:].indirect(n1_sb[:]), ACT.Copy)
+            nc.scalar.activation(y_near[t][:, 1, :], y_win[t][:].indirect(n2_sb[:]), ACT.Copy)
             nc.scalar.activation(dg, d_banks[t][:], ACT.Copy, scale=gs_sb[:, t : t + 1])
-            nc.scalar.activation(d_n3[:, t, :], d_win[t][:].indirect(n3_sb[:]), ACT.Copy)
-            nc.vector.tensor_tensor(diff1[:, t, :], y_n1, y, ALU.subtract)
-            nc.vector.tensor_tensor(diff2[:, t, :], y_n2[:, t, :], y, ALU.subtract)
-            nc.vector.tensor_tensor(term1[:, t, :], diff1[:, t, :], dg, ALU.mult)
-            nc.vector.scalar_tensor_tensor(term2[:, t, :], d_n3[:, t, :], 0.5, diff2[:, t, :], ALU.mult, ALU.mult)
-
-        z_bf = sb("z_bf", [P, S, PACK], BF16)
-        nc.vector.tensor_tensor(
-            z_bf[:].rearrange("p (c i) t -> p c t i", i=4),
-            term1[:].rearrange("p t (c i) -> p c t i", i=4),
-            term2[:].rearrange("p t (c i) -> p c t i", i=4),
-            ALU.add,
-        )
-        z_words = sb("z_words", [P, S], U32)
-        z_scales = sb("z_scales", [P, S], U8)
-        nc.vector.quantize_mx(out=z_words[:].bitcast(FP8X4), scales=z_scales[:], in_=z_bf[:].rearrange("p j t -> p (j t)"))
-
-        h_banks = []
+            nc.vector.tensor_tensor(diff[:, t, :, :], y_near[t][:], y.unsqueeze(1).broadcast_to([P, 2, S]), ALU.subtract)
+            nc.vector.tensor_tensor(term1[:, t, :], diff[:, t, 0, :], dg, ALU.mult)
         for t in range(PACK):
-            bank = psum.tile([P, S], F32, name=f"h_bank{t}", tag=f"y{t}")
-            nc.tensor.matmul_mx(
-                out=bank[:],
-                lhsT=code_dealt[:, P * t : P * (t + 1)].bitcast(FP8X4),
-                lhsT_scale=code_scale_dealt[:, P * t : P * (t + 1)],
-                rhs=z_words[:].bitcast(FP8X4),
-                rhs_scale=z_scales[:],
-                start=True,
-                stop=True,
-            )
-            h_banks.append(bank)
+            for cols in halves if t == PACK - 1 else [slice(0, S)]:
+                entries = n3_sb[:, cols.start // 16 : cols.stop // 16]
+                nc.scalar.activation(d_n3[t][:, cols], d_win[t][:].indirect(entries), ACT.Copy)
+                nc.vector.scalar_tensor_tensor(term2[:, t, cols], d_n3[t][:, cols], 0.5, diff[:, t, 1, cols], ALU.mult, ALU.mult)
 
-        e_n4 = sb("e_n4", [P, PACK, S], F32)
-        e_n5 = sb("e_n5", [P, PACK, S], F32)
-        part = sb("part", [P, PACK, S], F32)
-        total = sb("total", [P, PACK, S], F32)
-        root = sb("root", [P, PACK, S], F32)
-        half = sb("half", [P, PACK, S], F32)
+        h_banks = [psum.tile([P, S], F32, name=f"h_bank{t}", tag=f"y{t}") for t in range(PACK)]
+        for u, cols in enumerate(halves):
+            z_bf = sb(f"z_bf{u}", [P, S // 2, PACK], BF16)
+            nc.vector.tensor_tensor(
+                z_bf[:].rearrange("p (c i) t -> p c t i", i=4),
+                term1[:, :, cols].rearrange("p t (c i) -> p c t i", i=4),
+                term2[:, :, cols].rearrange("p t (c i) -> p c t i", i=4),
+                ALU.add,
+            )
+            z_words = sb(f"z_words{u}", [P, S // 2], U32)
+            z_scales = sb(f"z_scales{u}", [P, S // 2], U8)
+            nc.vector.quantize_mx(out=z_words[:].bitcast(FP8X4), scales=z_scales[:], in_=z_bf[:].rearrange("p j t -> p (j t)"))
+            for t in range(PACK):
+                nc.tensor.matmul_mx(
+                    out=h_banks[t][:, cols],
+                    lhsT=code_dealt[:, P * t : P * (t + 1)].bitcast(FP8X4),
+                    lhsT_scale=code_scale_dealt[:, P * t : P * (t + 1)],
+                    rhs=z_words[:].bitcast(FP8X4),
+                    rhs_scale=z_scales[:],
+                    start=True,
+                    stop=True,
+                )
+
+        def tiles(name):
+            return [sb(f"{name}{t}", [P, S], F32) for t in range(PACK)]
+
+        e_n4, near, total, root, factor = tiles("e_n4_"), tiles("near"), tiles("total"), tiles("root"), tiles("factor")
         result = sb("result", [P, PACK, S], F32)
         for t in range(PACK):
             nc.scalar.activation(e_win[t][:, :S], h_banks[t][:], ACT.Exp, scale=0.03125)
-        for t in range(PACK):
-            nc.vector.tensor_copy(e_n5[:, t, :], e_win[t][:].indirect(n5_sb[:]))
-            nc.scalar.activation(e_n4[:, t, :], e_win[t][:].indirect(n4_sb[:]), ACT.Copy)
-            nc.vector.tensor_tensor(part[:, t, :], e_n5[:, t, :], e_win[t][:, :S], ALU.add)
-        for t in range(PACK):
-            nc.vector.tensor_tensor(total[:, t, :], part[:, t, :], e_n4[:, t, :], ALU.add)
+            nc.scalar.activation(e_n4[t][:], e_win[t][:].indirect(n4_sb[:]), ACT.Copy)
+            nc.vector.tensor_tensor(near[t][:], e_win[t][:].indirect(n5_sb[:]), e_n4[t][:], ALU.add)
+            nc.vector.tensor_tensor(total[t][:], near[t][:], e_win[t][:, :S], ALU.add)
         out_rows = out_0.rearrange("(p t) j -> p t j", t=PACK)
         for t in range(PACK):
-            nc.scalar.activation(root[:, t, :], total[:, t, :], ACT.Abs_reciprocal_sqrt, scale=0.5)
-            nc.vector.tensor_tensor(half[:, t, :], root[:, t, :], e_win[t][:, :S], ALU.mult)
-            nc.vector.tensor_tensor(result[:, t, :], half[:, t, :], root[:, t, :], ALU.mult)
+            nc.scalar.activation(root[t][:], total[t][:], ACT.Abs_reciprocal_sqrt, scale=0.5)
+        for t in range(2):
+            nc.vector.tensor_tensor(factor[t][:], root[t][:], e_win[t][:, :S], ALU.mult)
+        for t in range(2):
+            nc.vector.tensor_tensor(result[:, t, :], factor[t][:], root[t][:], ALU.mult)
+        for t in range(2, PACK):
+            nc.scalar.activation(factor[t][:], root[t][:], ACT.Square)
+            nc.vector.tensor_tensor(result[:, t, :], factor[t][:], e_win[t][:, :S], ALU.mult)
+        for t in range(PACK):
             nc.sync.dma_start(out_rows[:, t, :], result[:, t, :])
 
         result_bf = sb("result_bf", [P, S, PACK], BF16)
+        split = 160
         nc.vector.tensor_copy(
-            result_bf[:].rearrange("p (c i) t -> p c t i", i=4),
-            result[:].rearrange("p t (c i) -> p c t i", i=4),
+            result_bf[:, :split, :].rearrange("p (c i) t -> p c t i", i=4),
+            result[:, :, :split].rearrange("p t (c i) -> p c t i", i=4),
+        )
+        nc.scalar.copy(
+            result_bf[:, split:, :].rearrange("p (c i) t -> p c t i", i=4),
+            result[:, :, split:].rearrange("p t (c i) -> p c t i", i=4),
         )
         out_words = sb("out_words", [P, S], U32)
         out_scales = sb("out_scales", [P, S], U8)

@@ -47,12 +47,6 @@ def tile_picked_twqflowbshare_none_po_kernel(
         w1_scale_raw = sb("w1_scale_raw", [P, H], U8)
         w2_scale_raw = keep.tile([P, H], U8, name="w2_scale_raw", tag="stage", align_bytes=64)
         d_scale_table = sb("d_scale_table", [P, G], U8)
-        nc.gpsimd.memset(d_scale_table[:].bitcast(I32), 0)
-
-        for e in range(2):
-            nc.gpsimd.dma_start(d_scale_table[e:P:16, :].bitcast(I32), d_scales[0, e:16:2, :].bitcast(I32))
-        gs_sb = sb("gs_sb", [P, PACK], F32)
-        nc.gpsimd.dma_start(gs_sb[:], gs.rearrange("(p t) o -> p (t o)", t=PACK))
 
         offs_sb = load_list("offs_sb", offs)
         w1_raw = sb("w1_raw", [P, 2 * H], U8)
@@ -62,14 +56,18 @@ def tile_picked_twqflowbshare_none_po_kernel(
         nc.sync.dma_start(x_table[:].bitcast(I32), x_words[0].rearrange("p n t -> p (n t)").bitcast(I32))
         two_sb = load_list("two_sb", two)
         load_scale_rows(nc.sync, w1_scale_raw, w1_scales)
-        w2_raw = sb("w2_raw", [P, 2 * H], U8)
-        nc.sync.dma_start(w2_raw[:].bitcast(I32), w2_words[0].bitcast(I32))
         n1_sb = load_list("n1_sb", n1)
         n2_sb = load_list("n2_sb", n2)
-        load_scale_rows(nc.sync, w2_scale_raw, w2_scales)
         k1_sb = load_list("k1_sb", k1)
+        rows = d_scales[0].bitcast(I32)
+        nc.sync.dma_start(d_scale_table[:].bitcast(I32), rows.unsqueeze(1).broadcast_to([16, 8, G // 4]))
+        w2_raw = sb("w2_raw", [P, 2 * H], U8)
+        nc.sync.dma_start(w2_raw[:].bitcast(I32), w2_words[0].bitcast(I32))
+        load_scale_rows(nc.sync, w2_scale_raw, w2_scales)
         d_table = sb("d_table", [P, G], U32)
         nc.sync.dma_start(d_table[:].bitcast(I32), d_words[0].rearrange("p n t -> p (n t)").bitcast(I32))
+        gs_sb = sb("gs_sb", [P, PACK], F32)
+        nc.sync.dma_start(gs_sb[:], gs.rearrange("(p t) o -> p (t o)", t=PACK))
         n3_sb = load_list("n3_sb", n3)
         n4_sb = load_list("n4_sb", n4)
         n5_sb = load_list("n5_sb", n5)
@@ -126,11 +124,7 @@ def tile_picked_twqflowbshare_none_po_kernel(
         y_banks = project("y", w1_dealt, w1_scale_dealt, xq_words, xq_scales)
         x2_scales = pick("x2_scales", x_scale_table, two_sb, S, U8)
         x2_words = pick("x2_words", x_table, two_sb, S, U32)
-        w2_dealt = deal_words("w2_dealt", w2_raw)
-        w2_scale_dealt = deal("w2_scale_dealt", w2_scale_raw, U8)
-        d_banks = project("d", w2_dealt, w2_scale_dealt, x2_words, x2_scales)
-
-        code_scale_picked = keep.tile([P, H], U8, name="code_scale_picked", tag="stage", align_bytes=64)
+        code_scale_picked = sb("code_scale_picked", [P, H], U8)
         code_dealt = sb("code_dealt", [P, H], U32)
         code_scale_dealt = sb("code_scale_dealt", [P, H], U8)
         nc.vector.tensor_copy(code_scale_picked[:], d_scale_table[:].indirect(k1_sb[:]))
@@ -138,35 +132,52 @@ def tile_picked_twqflowbshare_none_po_kernel(
             code_scale_dealt[:].rearrange("p (t m) -> p t m", t=PACK),
             code_scale_picked[:].rearrange("p (m t) -> p t m", t=PACK),
         )
-        for e in range(2):
-            nc.sync.dma_start(code_scale_dealt[2 + e : P : 32, :].bitcast(I32), code_scale_dealt[16 + e : P : 32, :].bitcast(I32))
-        code_picked = keep.tile([P, H], U32, name="code_picked", tag="stage", align_bytes=64)
+        for r in range(1, 4):
+            nc.sync.dma_start(code_scale_dealt[r:P:32, :].bitcast(I32), code_scale_dealt[8 * r : P : 32, :].bitcast(I32))
+        w2_dealt = deal_words("w2_dealt", w2_raw)
+        w2_scale_dealt = deal("w2_scale_dealt", w2_scale_raw, U8)
+        d_banks = project("d", w2_dealt, w2_scale_dealt, x2_words, x2_scales)
+
+
+        def staged(name, shape, dtype, tag):
+            return keep.tile(shape, dtype, name=name, tag=tag, align_bytes=64)
+
+        d_n3 = [sb(f"d_n3_{t}", [P, S], F32) for t in range(PACK)]
+        term1 = sb("term1", [P, PACK, S], F32)
+        term2 = sb("term2", [P, PACK, S], F32)
+        halves = [slice(0, S // 2), slice(S // 2, S)]
+        diff = []
+
+        def differences(row_tiles, tag):
+            both = staged(f"diff{row_tiles[0]}", [P, len(row_tiles), 2, S], F32, tag)
+            for i, t in enumerate(row_tiles):
+                y = y_win[t][:, :S]
+                dg = d_win[t][:, :S]
+                y_near = staged(f"y_near{t}", [P, 2, S], F32, "stage2" if t == 1 else f"y_near{t}")
+                nc.scalar.activation(y, y_banks[t][:], ACT.Copy)
+                nc.scalar.activation(y_near[:, 0, :], y_win[t][:].indirect(n1_sb[:]), ACT.Copy)
+                nc.scalar.activation(y_near[:, 1, :], y_win[t][:].indirect(n2_sb[:]), ACT.Copy)
+                if t < 2:
+                    nc.vector.tensor_scalar(dg, d_banks[t][:], gs_sb[:, t : t + 1], None, ALU.mult)
+                else:
+                    nc.scalar.activation(dg, d_banks[t][:], ACT.Copy, scale=gs_sb[:, t : t + 1])
+                nc.vector.tensor_tensor(both[:, i, :, :], y_near[:], y.unsqueeze(1).broadcast_to([P, 2, S]), ALU.subtract)
+                nc.vector.tensor_tensor(term1[:, t, :], both[:, i, 0, :], dg, ALU.mult)
+                diff.append(both[:, i, 1, :])
+
+        differences([0, 1], "stage")
+        code_picked = staged("code_picked", [P, H], U32, "stage2")
         nc.vector.tensor_copy(code_picked[:], d_table[:].indirect(k1_sb[:]))
         nc.vector.tensor_copy(
             code_dealt[:].rearrange("p (t m) -> p t m", t=PACK),
             code_picked[:].rearrange("p (m t) -> p t m", t=PACK),
         )
-
-        y_near = [sb(f"y_near{t}", [P, 2, S], F32) for t in range(PACK)]
-        d_n3 = [sb(f"d_n3_{t}", [P, S], F32) for t in range(PACK)]
-        diff = keep.tile([P, PACK, 2, S], F32, name="diff", tag="stage", align_bytes=64)
-        term1 = sb("term1", [P, PACK, S], F32)
-        term2 = sb("term2", [P, PACK, S], F32)
-        halves = [slice(0, S // 2), slice(S // 2, S)]
-        for t in range(PACK):
-            y = y_win[t][:, :S]
-            dg = d_win[t][:, :S]
-            nc.scalar.activation(y, y_banks[t][:], ACT.Copy)
-            nc.scalar.activation(y_near[t][:, 0, :], y_win[t][:].indirect(n1_sb[:]), ACT.Copy)
-            nc.scalar.activation(y_near[t][:, 1, :], y_win[t][:].indirect(n2_sb[:]), ACT.Copy)
-            nc.scalar.activation(dg, d_banks[t][:], ACT.Copy, scale=gs_sb[:, t : t + 1])
-            nc.vector.tensor_tensor(diff[:, t, :, :], y_near[t][:], y.unsqueeze(1).broadcast_to([P, 2, S]), ALU.subtract)
-            nc.vector.tensor_tensor(term1[:, t, :], diff[:, t, 0, :], dg, ALU.mult)
+        differences([2, 3], "stage2")
         for t in range(PACK):
             for cols in halves if t == PACK - 1 else [slice(0, S)]:
                 entries = n3_sb[:, cols.start // 16 : cols.stop // 16]
                 nc.scalar.activation(d_n3[t][:, cols], d_win[t][:].indirect(entries), ACT.Copy)
-                nc.vector.scalar_tensor_tensor(term2[:, t, cols], d_n3[t][:, cols], 0.5, diff[:, t, 1, cols], ALU.mult, ALU.mult)
+                nc.vector.scalar_tensor_tensor(term2[:, t, cols], d_n3[t][:, cols], 0.5, diff[t][:, cols], ALU.mult, ALU.mult)
 
         h_banks = [psum.tile([P, S], F32, name=f"h_bank{t}", tag=f"y{t}") for t in range(PACK)]
         for u, cols in enumerate(halves):

@@ -83,16 +83,16 @@ def tile_picked_twqflowbshare_none_po_kernel(
         def deal_words(name, w_raw):
             dealt = sb(name, [P, 2 * H], U8)
             nc.vector.tensor_copy(
-                dealt[:].bitcast(U16).rearrange("p (t m) -> p t m", t=PACK),
-                w_raw[:].bitcast(U16).rearrange("p (m t) -> p t m", t=PACK),
+                dealt[:].bitcast(U16).rearrange("p (t c i) -> p c t i", t=PACK, i=8),
+                w_raw[:].bitcast(U16).rearrange("p (c i t) -> p c t i", t=PACK, i=8),
             )
             return dealt
 
         def deal(name, raw, dtype):
             dealt = sb(name, [P, H], dtype)
             nc.vector.tensor_copy(
-                dealt[:].rearrange("p (t m) -> p t m", t=PACK),
-                raw[:].rearrange("p (m t) -> p t m", t=PACK),
+                dealt[:].rearrange("p (t c i) -> p c t i", t=PACK, i=16),
+                raw[:].rearrange("p (c i t) -> p c t i", t=PACK, i=16),
             )
             return dealt
 
@@ -129,8 +129,8 @@ def tile_picked_twqflowbshare_none_po_kernel(
         code_scale_dealt = sb("code_scale_dealt", [P, H], U8)
         nc.vector.tensor_copy(code_scale_picked[:], d_scale_table[:].indirect(k1_sb[:]))
         nc.vector.tensor_copy(
-            code_scale_dealt[:].rearrange("p (t m) -> p t m", t=PACK),
-            code_scale_picked[:].rearrange("p (m t) -> p t m", t=PACK),
+            code_scale_dealt[:].rearrange("p (t c i) -> p c t i", t=PACK, i=16),
+            code_scale_picked[:].rearrange("p (c i t) -> p c t i", t=PACK, i=16),
         )
         for r in range(1, 4):
             nc.sync.dma_start(code_scale_dealt[r:P:32, :].bitcast(I32), code_scale_dealt[8 * r : P : 32, :].bitcast(I32))
@@ -157,10 +157,7 @@ def tile_picked_twqflowbshare_none_po_kernel(
                 nc.scalar.activation(y, y_banks[t][:], ACT.Copy)
                 nc.scalar.activation(y_near[:, 0, :], y_win[t][:].indirect(n1_sb[:]), ACT.Copy)
                 nc.scalar.activation(y_near[:, 1, :], y_win[t][:].indirect(n2_sb[:]), ACT.Copy)
-                if t < 2:
-                    nc.vector.tensor_scalar(dg, d_banks[t][:], gs_sb[:, t : t + 1], None, ALU.mult)
-                else:
-                    nc.scalar.activation(dg, d_banks[t][:], ACT.Copy, scale=gs_sb[:, t : t + 1])
+                nc.scalar.activation(dg, d_banks[t][:], ACT.Copy, scale=gs_sb[:, t : t + 1])
                 nc.vector.tensor_tensor(both[:, i, :, :], y_near[:], y.unsqueeze(1).broadcast_to([P, 2, S]), ALU.subtract)
                 nc.vector.tensor_tensor(term1[:, t, :], both[:, i, 0, :], dg, ALU.mult)
                 diff.append(both[:, i, 1, :])
@@ -169,8 +166,8 @@ def tile_picked_twqflowbshare_none_po_kernel(
         code_picked = staged("code_picked", [P, H], U32, "stage2")
         nc.vector.tensor_copy(code_picked[:], d_table[:].indirect(k1_sb[:]))
         nc.vector.tensor_copy(
-            code_dealt[:].rearrange("p (t m) -> p t m", t=PACK),
-            code_picked[:].rearrange("p (m t) -> p t m", t=PACK),
+            code_dealt[:].rearrange("p (t c i) -> p c t i", t=PACK, i=4),
+            code_picked[:].rearrange("p (c i t) -> p c t i", t=PACK, i=4),
         )
         differences([2, 3], "stage2")
         for t in range(PACK):

@@ -18,7 +18,16 @@ ALU = mybir.AluOpType
 
 P = 128
 PACK = 4
-WIN = 2 * S
+QUADRANT = 32
+BLOCK_PARTITIONS = 8
+LIST_ROWS = 16
+LINE = 16
+EIGHT_LIST_WINDOW = 2 * S
+ONE_LIST_WINDOW = S + LIST_ROWS
+H_TO_EXPONENT = 0.0625 * 0.5
+D_COPIES_ON_VECTOR = 1
+SQUARES_ON_VECTOR = 2
+CAST_COLUMNS_ON_VECTOR = 160
 
 
 def tile_picked_twqflowbshare_none_po_kernel(
@@ -30,74 +39,84 @@ def tile_picked_twqflowbshare_none_po_kernel(
         keep = ctx.enter_context(tc.tile_pool(name="keep", bufs=1))
         psum = ctx.enter_context(tc.psum_pool(name="psum", bufs=1))
 
-        def sb(name, shape, dtype):
-            return keep.tile(shape, dtype, name=name, align_bytes=64)
+        def sb(name, shape, dtype, buffer=None):
+            return keep.tile(shape, dtype, name=name, tag=buffer or name, align_bytes=64)
 
         def load_list(name, src):
             tile = keep.tile(list(src.shape), U16, name=name)
             nc.sync.dma_start(tile[:], src)
             return tile
 
-        def load_scale_rows(queue, tile, scales):
-            for q in range(4):
+        def load_scale_rows(tile, scales):
+            for q in range(P // QUADRANT):
                 rows = scales[0, 4 * q : 4 * q + 4, :].bitcast(I32)
-                queue.dma_start(tile[32 * q : 32 * q + 32, :].bitcast(I32), rows.unsqueeze(0).broadcast_to([8, *rows.shape]))
+                repeated = rows.unsqueeze(0).broadcast_to([QUADRANT // 4, *rows.shape])
+                nc.sync.dma_start(tile[QUADRANT * q : QUADRANT * (q + 1), :].bitcast(I32), repeated)
+
+        def deal(dealt, raw, element_bytes):
+            run = LINE // element_bytes
+            nc.vector.tensor_copy(
+                dealt.rearrange("p (t c i) -> p c t i", t=PACK, i=run),
+                raw.rearrange("p (c i t) -> p c t i", t=PACK, i=run),
+            )
+
+        def by_word(ap):
+            return ap.rearrange("p (c i) t -> p c t i", i=4)
+
+        def by_row_tile(ap):
+            return ap.rearrange("p t (c i) -> p c t i", i=4)
+
+        after_w2, after_tile_1 = "after_w2", "after_tile_1"
 
         x_scale_table = sb("x_scale_table", [P, T], U8)
         w1_scale_raw = sb("w1_scale_raw", [P, H], U8)
-        w2_scale_raw = keep.tile([P, H], U8, name="w2_scale_raw", tag="stage", align_bytes=64)
-        d_scale_table = sb("d_scale_table", [P, G], U8)
+        w2_scale_raw = sb("w2_scale_raw", [P, H], U8, after_w2)
+        dict_scale_table = sb("dict_scale_table", [P, G], U8)
 
         offs_sb = load_list("offs_sb", offs)
         w1_raw = sb("w1_raw", [P, 2 * H], U8)
         nc.sync.dma_start(w1_raw[:].bitcast(I32), w1_words[0].bitcast(I32))
-        load_scale_rows(nc.sync, x_scale_table, x_scales)
+        load_scale_rows(x_scale_table, x_scales)
         x_table = sb("x_table", [P, T], U32)
         nc.sync.dma_start(x_table[:].bitcast(I32), x_words[0].rearrange("p n t -> p (n t)").bitcast(I32))
+        load_scale_rows(w1_scale_raw, w1_scales)
         two_sb = load_list("two_sb", two)
-        load_scale_rows(nc.sync, w1_scale_raw, w1_scales)
         n1_sb = load_list("n1_sb", n1)
         n2_sb = load_list("n2_sb", n2)
         k1_sb = load_list("k1_sb", k1)
-        rows = d_scales[0].bitcast(I32)
-        nc.sync.dma_start(d_scale_table[:].bitcast(I32), rows.unsqueeze(1).broadcast_to([16, 8, G // 4]))
+        dict_rows = d_scales[0].bitcast(I32).unsqueeze(1).broadcast_to([P // BLOCK_PARTITIONS, BLOCK_PARTITIONS, G // 4])
+        nc.sync.dma_start(dict_scale_table[:].bitcast(I32), dict_rows)
         w2_raw = sb("w2_raw", [P, 2 * H], U8)
         nc.sync.dma_start(w2_raw[:].bitcast(I32), w2_words[0].bitcast(I32))
-        load_scale_rows(nc.sync, w2_scale_raw, w2_scales)
-        d_table = sb("d_table", [P, G], U32)
-        nc.sync.dma_start(d_table[:].bitcast(I32), d_words[0].rearrange("p n t -> p (n t)").bitcast(I32))
+        load_scale_rows(w2_scale_raw, w2_scales)
+        dict_table = sb("dict_table", [P, G], U32)
+        nc.sync.dma_start(dict_table[:].bitcast(I32), d_words[0].rearrange("p n t -> p (n t)").bitcast(I32))
         gs_sb = sb("gs_sb", [P, PACK], F32)
         nc.sync.dma_start(gs_sb[:], gs.rearrange("(p t) o -> p (t o)", t=PACK))
         n3_sb = load_list("n3_sb", n3)
         n4_sb = load_list("n4_sb", n4)
         n5_sb = load_list("n5_sb", n5)
 
-        y_win = [sb(f"y_win{t}", [P, WIN], F32) for t in range(PACK)]
-        d_win = [sb(f"d_win{t}", [P, WIN], F32) for t in range(PACK)]
-        e_win = [sb(f"e_win{t}", [P, S + 16], F32) for t in range(PACK)]
+        y_win = [sb(f"y_win{t}", [P, EIGHT_LIST_WINDOW], F32) for t in range(PACK)]
+        d_win = [sb(f"d_win{t}", [P, EIGHT_LIST_WINDOW], F32) for t in range(PACK)]
+        e_win = [sb(f"e_win{t}", [P, ONE_LIST_WINDOW], F32) for t in range(PACK)]
         for t in range(PACK):
             nc.vector.memset(y_win[t][:, S:], 0.0)
             nc.scalar.activation(d_win[t][:, S:], y_win[t][:, S:], ACT.Copy)
             nc.vector.memset(e_win[t][:, S:], 0.0)
 
-        def deal_words(name, w_raw):
+        def deal_weight_words(name, w_raw):
             dealt = sb(name, [P, 2 * H], U8)
-            nc.vector.tensor_copy(
-                dealt[:].bitcast(U16).rearrange("p (t c i) -> p c t i", t=PACK, i=8),
-                w_raw[:].bitcast(U16).rearrange("p (c i t) -> p c t i", t=PACK, i=8),
-            )
+            deal(dealt[:].bitcast(U16), w_raw[:].bitcast(U16), 2)
             return dealt
 
-        def deal(name, raw, dtype):
-            dealt = sb(name, [P, H], dtype)
-            nc.vector.tensor_copy(
-                dealt[:].rearrange("p (t c i) -> p c t i", t=PACK, i=16),
-                raw[:].rearrange("p (c i t) -> p c t i", t=PACK, i=16),
-            )
+        def deal_scales(name, raw):
+            dealt = sb(name, [P, H], U8)
+            deal(dealt[:], raw[:], 1)
             return dealt
 
-        def pick(name, table, offsets, count, dtype):
-            picked = sb(name, [P, count], dtype)
+        def pick(name, table, offsets, count, dtype, buffer=None):
+            picked = sb(name, [P, count], dtype, buffer)
             nc.vector.tensor_copy(picked[:], table[:].indirect(offsets[:]))
             return picked
 
@@ -117,125 +136,109 @@ def tile_picked_twqflowbshare_none_po_kernel(
                 banks.append(bank)
             return banks
 
-        w1_dealt = deal_words("w1_dealt", w1_raw)
-        xq_scales = pick("xq_scales", x_scale_table, offs_sb, S, U8)
-        xq_words = pick("xq_words", x_table, offs_sb, S, U32)
-        w1_scale_dealt = deal("w1_scale_dealt", w1_scale_raw, U8)
-        y_banks = project("y", w1_dealt, w1_scale_dealt, xq_words, xq_scales)
-        x2_scales = pick("x2_scales", x_scale_table, two_sb, S, U8)
-        x2_words = pick("x2_words", x_table, two_sb, S, U32)
-        code_scale_picked = sb("code_scale_picked", [P, H], U8)
-        code_dealt = sb("code_dealt", [P, H], U32)
-        code_scale_dealt = sb("code_scale_dealt", [P, H], U8)
-        nc.vector.tensor_copy(code_scale_picked[:], d_scale_table[:].indirect(k1_sb[:]))
-        nc.vector.tensor_copy(
-            code_scale_dealt[:].rearrange("p (t c i) -> p c t i", t=PACK, i=16),
-            code_scale_picked[:].rearrange("p (c i t) -> p c t i", t=PACK, i=16),
-        )
+        w1_dealt = deal_weight_words("w1_dealt", w1_raw)
+        x_idx_scales = pick("x_idx_scales", x_scale_table, offs_sb, S, U8)
+        x_idx_words = pick("x_idx_words", x_table, offs_sb, S, U32)
+        w1_scale_dealt = deal_scales("w1_scale_dealt", w1_scale_raw)
+        y_banks = project("y", w1_dealt, w1_scale_dealt, x_idx_words, x_idx_scales)
+        x_two_scales = pick("x_two_scales", x_scale_table, two_sb, S, U8)
+        x_two_words = pick("x_two_words", x_table, two_sb, S, U32)
+
+        dict_scale_picked = pick("dict_scale_picked", dict_scale_table, k1_sb, H, U8)
+        dict_dealt = sb("dict_dealt", [P, H], U32)
+        dict_scale_dealt = deal_scales("dict_scale_dealt", dict_scale_picked)
         for r in range(1, 4):
-            nc.sync.dma_start(code_scale_dealt[r:P:32, :].bitcast(I32), code_scale_dealt[8 * r : P : 32, :].bitcast(I32))
-        w2_dealt = deal_words("w2_dealt", w2_raw)
-        w2_scale_dealt = deal("w2_scale_dealt", w2_scale_raw, U8)
-        d_banks = project("d", w2_dealt, w2_scale_dealt, x2_words, x2_scales)
+            nc.sync.dma_start(
+                dict_scale_dealt[r:P:QUADRANT, :].bitcast(I32),
+                dict_scale_dealt[BLOCK_PARTITIONS * r : P : QUADRANT, :].bitcast(I32),
+            )
 
-
-        def staged(name, shape, dtype, tag):
-            return keep.tile(shape, dtype, name=name, tag=tag, align_bytes=64)
+        w2_dealt = deal_weight_words("w2_dealt", w2_raw)
+        w2_scale_dealt = deal_scales("w2_scale_dealt", w2_scale_raw)
+        d_banks = project("d", w2_dealt, w2_scale_dealt, x_two_words, x_two_scales)
 
         d_n3 = [sb(f"d_n3_{t}", [P, S], F32) for t in range(PACK)]
         term1 = sb("term1", [P, PACK, S], F32)
         term2 = sb("term2", [P, PACK, S], F32)
         halves = [slice(0, S // 2), slice(S // 2, S)]
-        diff = []
+        diff_n2 = []
 
-        def differences(row_tiles, tag):
-            both = staged(f"diff{row_tiles[0]}", [P, len(row_tiles), 2, S], F32, tag)
+        def differences(row_tiles, buffer):
+            diffs = sb(f"diffs{row_tiles[0]}", [P, len(row_tiles), 2, S], F32, buffer)
             for i, t in enumerate(row_tiles):
                 y = y_win[t][:, :S]
-                dg = d_win[t][:, :S]
-                y_near = staged(f"y_near{t}", [P, 2, S], F32, "stage2" if t == 1 else f"y_near{t}")
+                gs_d = d_win[t][:, :S]
+                y_near = sb(f"y_near{t}", [P, 2, S], F32, after_tile_1 if t == 1 else None)
                 nc.scalar.activation(y, y_banks[t][:], ACT.Copy)
                 nc.scalar.activation(y_near[:, 0, :], y_win[t][:].indirect(n1_sb[:]), ACT.Copy)
                 nc.scalar.activation(y_near[:, 1, :], y_win[t][:].indirect(n2_sb[:]), ACT.Copy)
-                nc.scalar.activation(dg, d_banks[t][:], ACT.Copy, scale=gs_sb[:, t : t + 1])
-                nc.vector.tensor_tensor(both[:, i, :, :], y_near[:], y.unsqueeze(1).broadcast_to([P, 2, S]), ALU.subtract)
-                nc.vector.tensor_tensor(term1[:, t, :], both[:, i, 0, :], dg, ALU.mult)
-                diff.append(both[:, i, 1, :])
+                if t < D_COPIES_ON_VECTOR:
+                    nc.vector.tensor_scalar(gs_d, d_banks[t][:], gs_sb[:, t : t + 1], None, ALU.mult)
+                else:
+                    nc.scalar.activation(gs_d, d_banks[t][:], ACT.Copy, scale=gs_sb[:, t : t + 1])
+                nc.vector.tensor_tensor(diffs[:, i, :, :], y_near[:], y.unsqueeze(1).broadcast_to([P, 2, S]), ALU.subtract)
+                nc.vector.tensor_tensor(term1[:, t, :], diffs[:, i, 0, :], gs_d, ALU.mult)
+                diff_n2.append(diffs[:, i, 1, :])
 
-        differences([0, 1], "stage")
-        code_picked = staged("code_picked", [P, H], U32, "stage2")
-        nc.vector.tensor_copy(code_picked[:], d_table[:].indirect(k1_sb[:]))
-        nc.vector.tensor_copy(
-            code_dealt[:].rearrange("p (t c i) -> p c t i", t=PACK, i=4),
-            code_picked[:].rearrange("p (c i t) -> p c t i", t=PACK, i=4),
-        )
-        differences([2, 3], "stage2")
+        differences([0, 1], after_w2)
+        dict_picked = pick("dict_picked", dict_table, k1_sb, H, U32, after_tile_1)
+        deal(dict_dealt[:], dict_picked[:], 4)
+        differences([2, 3], after_tile_1)
+
         for t in range(PACK):
             for cols in halves if t == PACK - 1 else [slice(0, S)]:
-                entries = n3_sb[:, cols.start // 16 : cols.stop // 16]
+                entries = n3_sb[:, cols.start // LIST_ROWS : cols.stop // LIST_ROWS]
                 nc.scalar.activation(d_n3[t][:, cols], d_win[t][:].indirect(entries), ACT.Copy)
-                nc.vector.scalar_tensor_tensor(term2[:, t, cols], d_n3[t][:, cols], 0.5, diff[t][:, cols], ALU.mult, ALU.mult)
+                nc.vector.scalar_tensor_tensor(term2[:, t, cols], d_n3[t][:, cols], 0.5, diff_n2[t][:, cols], ALU.mult, ALU.mult)
 
         h_banks = [psum.tile([P, S], F32, name=f"h_bank{t}", tag=f"y{t}") for t in range(PACK)]
         for u, cols in enumerate(halves):
             z_bf = sb(f"z_bf{u}", [P, S // 2, PACK], BF16)
-            nc.vector.tensor_tensor(
-                z_bf[:].rearrange("p (c i) t -> p c t i", i=4),
-                term1[:, :, cols].rearrange("p t (c i) -> p c t i", i=4),
-                term2[:, :, cols].rearrange("p t (c i) -> p c t i", i=4),
-                ALU.add,
-            )
+            nc.vector.tensor_tensor(by_word(z_bf[:]), by_row_tile(term1[:, :, cols]), by_row_tile(term2[:, :, cols]), ALU.add)
             z_words = sb(f"z_words{u}", [P, S // 2], U32)
             z_scales = sb(f"z_scales{u}", [P, S // 2], U8)
             nc.vector.quantize_mx(out=z_words[:].bitcast(FP8X4), scales=z_scales[:], in_=z_bf[:].rearrange("p j t -> p (j t)"))
             for t in range(PACK):
                 nc.tensor.matmul_mx(
                     out=h_banks[t][:, cols],
-                    lhsT=code_dealt[:, P * t : P * (t + 1)].bitcast(FP8X4),
-                    lhsT_scale=code_scale_dealt[:, P * t : P * (t + 1)],
+                    lhsT=dict_dealt[:, P * t : P * (t + 1)].bitcast(FP8X4),
+                    lhsT_scale=dict_scale_dealt[:, P * t : P * (t + 1)],
                     rhs=z_words[:].bitcast(FP8X4),
                     rhs_scale=z_scales[:],
                     start=True,
                     stop=True,
                 )
 
-        def tiles(name):
+        def row_tiles_of(name):
             return [sb(f"{name}{t}", [P, S], F32) for t in range(PACK)]
 
-        e_n4, near, total, root, factor = tiles("e_n4_"), tiles("near"), tiles("total"), tiles("root"), tiles("factor")
+        e_n4, near, total, root, factor = (row_tiles_of(name) for name in ("e_n4_", "near", "total", "root", "factor"))
         result = sb("result", [P, PACK, S], F32)
         for t in range(PACK):
-            nc.scalar.activation(e_win[t][:, :S], h_banks[t][:], ACT.Exp, scale=0.03125)
+            nc.scalar.activation(e_win[t][:, :S], h_banks[t][:], ACT.Exp, scale=H_TO_EXPONENT)
             nc.scalar.activation(e_n4[t][:], e_win[t][:].indirect(n4_sb[:]), ACT.Copy)
             nc.vector.tensor_tensor(near[t][:], e_win[t][:].indirect(n5_sb[:]), e_n4[t][:], ALU.add)
             nc.vector.tensor_tensor(total[t][:], near[t][:], e_win[t][:, :S], ALU.add)
-        out_rows = out_0.rearrange("(p t) j -> p t j", t=PACK)
         for t in range(PACK):
             nc.scalar.activation(root[t][:], total[t][:], ACT.Abs_reciprocal_sqrt, scale=0.5)
-        for t in range(2):
+        for t in range(SQUARES_ON_VECTOR):
             nc.vector.tensor_tensor(factor[t][:], root[t][:], e_win[t][:, :S], ALU.mult)
-        for t in range(2):
+        for t in range(SQUARES_ON_VECTOR):
             nc.vector.tensor_tensor(result[:, t, :], factor[t][:], root[t][:], ALU.mult)
-        for t in range(2, PACK):
+        for t in range(SQUARES_ON_VECTOR, PACK):
             nc.scalar.activation(factor[t][:], root[t][:], ACT.Square)
             nc.vector.tensor_tensor(result[:, t, :], factor[t][:], e_win[t][:, :S], ALU.mult)
+        out_rows = out_0.rearrange("(p t) j -> p t j", t=PACK)
         for t in range(PACK):
             nc.sync.dma_start(out_rows[:, t, :], result[:, t, :])
 
         result_bf = sb("result_bf", [P, S, PACK], BF16)
-        split = 160
-        nc.vector.tensor_copy(
-            result_bf[:, :split, :].rearrange("p (c i) t -> p c t i", i=4),
-            result[:, :, :split].rearrange("p t (c i) -> p c t i", i=4),
-        )
-        nc.scalar.copy(
-            result_bf[:, split:, :].rearrange("p (c i) t -> p c t i", i=4),
-            result[:, :, split:].rearrange("p t (c i) -> p c t i", i=4),
-        )
+        nc.vector.tensor_copy(by_word(result_bf[:, :CAST_COLUMNS_ON_VECTOR, :]), by_row_tile(result[:, :, :CAST_COLUMNS_ON_VECTOR]))
+        nc.scalar.copy(by_word(result_bf[:, CAST_COLUMNS_ON_VECTOR:, :]), by_row_tile(result[:, :, CAST_COLUMNS_ON_VECTOR:]))
         out_words = sb("out_words", [P, S], U32)
         out_scales = sb("out_scales", [P, S], U8)
         nc.vector.quantize_mx(out=out_words[:].bitcast(FP8X4), scales=out_scales[:], in_=result_bf[:].rearrange("p j t -> p (j t)"))
         nc.sync.dma_start(out_1[0].rearrange("p n t -> p (n t)").bitcast(I32), out_words[:].bitcast(I32))
-        for q in range(4):
+        for q in range(P // QUADRANT):
             queue = nc.scalar if q % 2 == 0 else nc.sync
-            queue.dma_start(out_2[0, 4 * q : 4 * q + 4, :].bitcast(I32), out_scales[32 * q : 32 * q + 4, :].bitcast(I32))
+            queue.dma_start(out_2[0, 4 * q : 4 * q + 4, :].bitcast(I32), out_scales[QUADRANT * q : QUADRANT * q + 4, :].bitcast(I32))

from contextlib import ExitStack

import concourse.mybir as mybir

K, T, S, H, G = 512, 1024, 256, 512, 2048
FLOPS = 3 * 2 * K * H * S

F32 = mybir.dt.float32
BF16 = mybir.dt.bfloat16
I32 = mybir.dt.int32
U32 = mybir.dt.uint32
U16 = mybir.dt.uint16
U8 = mybir.dt.uint8
FP8X4 = mybir.dt.float8_e4m3fn_x4
FP4X4 = mybir.dt.float4_e2m1fn_x4
ACT = mybir.ActivationFunctionType
ALU = mybir.AluOpType

P = 128
PACK = 4
QUADRANT = 32
BLOCK_PARTITIONS = 8
LIST_ROWS = 16
LINE = 16
EIGHT_LIST_WINDOW = 2 * S
ONE_LIST_WINDOW = S + LIST_ROWS
H_TO_EXPONENT = 0.0625 * 0.5
D_COPIES_ON_VECTOR = 1
SQUARES_ON_VECTOR = 2
CAST_COLUMNS_ON_VECTOR = 160


def tile_picked_twqflowbshare_none_po_kernel(
    tc, x_words, x_scales, w1_words, w1_scales, w2_words, w2_scales, gs, d_words, d_scales,
    offs, two, n1, n2, n3, k1, n4, n5, out_0, out_1, out_2,
):
    nc = tc.nc
    with ExitStack() as ctx:
        keep = ctx.enter_context(tc.tile_pool(name="keep", bufs=1))
        psum = ctx.enter_context(tc.psum_pool(name="psum", bufs=1))

        def sb(name, shape, dtype, buffer=None):
            return keep.tile(shape, dtype, name=name, tag=buffer or name, align_bytes=64)

        def load_list(name, src):
            tile = keep.tile(list(src.shape), U16, name=name)
            nc.sync.dma_start(tile[:], src)
            return tile

        def load_scale_rows(tile, scales):
            for q in range(P // QUADRANT):
                rows = scales[0, 4 * q : 4 * q + 4, :].bitcast(I32)
                repeated = rows.unsqueeze(0).broadcast_to([QUADRANT // 4, *rows.shape])
                nc.sync.dma_start(tile[QUADRANT * q : QUADRANT * (q + 1), :].bitcast(I32), repeated)

        def deal(dealt, raw, element_bytes):
            run = LINE // element_bytes
            nc.vector.tensor_copy(
                dealt.rearrange("p (t c i) -> p c t i", t=PACK, i=run),
                raw.rearrange("p (c i t) -> p c t i", t=PACK, i=run),
            )

        def by_word(ap):
            return ap.rearrange("p (c i) t -> p c t i", i=4)

        def by_row_tile(ap):
            return ap.rearrange("p t (c i) -> p c t i", i=4)

        after_w2, after_tile_1 = "after_w2", "after_tile_1"

        x_scale_table = sb("x_scale_table", [P, T], U8)
        w1_scale_raw = sb("w1_scale_raw", [P, H], U8)
        w2_scale_raw = sb("w2_scale_raw", [P, H], U8, after_w2)
        dict_scale_table = sb("dict_scale_table", [P, G], U8)

        offs_sb = load_list("offs_sb", offs)
        w1_raw = sb("w1_raw", [P, 2 * H], U8)
        nc.sync.dma_start(w1_raw[:].bitcast(I32), w1_words[0].bitcast(I32))
        load_scale_rows(x_scale_table, x_scales)
        x_table = sb("x_table", [P, T], U32)
        nc.sync.dma_start(x_table[:].bitcast(I32), x_words[0].rearrange("p n t -> p (n t)").bitcast(I32))
        load_scale_rows(w1_scale_raw, w1_scales)
        two_sb = load_list("two_sb", two)
        n1_sb = load_list("n1_sb", n1)
        n2_sb = load_list("n2_sb", n2)
        k1_sb = load_list("k1_sb", k1)
        dict_rows = d_scales[0].bitcast(I32).unsqueeze(1).broadcast_to([P // BLOCK_PARTITIONS, BLOCK_PARTITIONS, G // 4])
        nc.sync.dma_start(dict_scale_table[:].bitcast(I32), dict_rows)
        w2_raw = sb("w2_raw", [P, 2 * H], U8)
        nc.sync.dma_start(w2_raw[:].bitcast(I32), w2_words[0].bitcast(I32))
        load_scale_rows(w2_scale_raw, w2_scales)
        dict_table = sb("dict_table", [P, G], U32)
        nc.sync.dma_start(dict_table[:].bitcast(I32), d_words[0].rearrange("p n t -> p (n t)").bitcast(I32))
        gs_sb = sb("gs_sb", [P, PACK], F32)
        nc.sync.dma_start(gs_sb[:], gs.rearrange("(p t) o -> p (t o)", t=PACK))
        n3_sb = load_list("n3_sb", n3)
        n4_sb = load_list("n4_sb", n4)
        n5_sb = load_list("n5_sb", n5)

        y_win = [sb(f"y_win{t}", [P, EIGHT_LIST_WINDOW], F32) for t in range(PACK)]
        d_win = [sb(f"d_win{t}", [P, EIGHT_LIST_WINDOW], F32) for t in range(PACK)]
        e_win = [sb(f"e_win{t}", [P, ONE_LIST_WINDOW], F32) for t in range(PACK)]
        for t in range(PACK):
            nc.vector.memset(y_win[t][:, S:], 0.0)
            nc.scalar.activation(d_win[t][:, S:], y_win[t][:, S:], ACT.Copy)
            nc.vector.memset(e_win[t][:, S:], 0.0)

        def deal_weight_words(name, w_raw):
            dealt = sb(name, [P, 2 * H], U8)
            deal(dealt[:].bitcast(U16), w_raw[:].bitcast(U16), 2)
            return dealt

        def deal_scales(name, raw):
            dealt = sb(name, [P, H], U8)
            deal(dealt[:], raw[:], 1)
            return dealt

        def pick(name, table, offsets, count, dtype, buffer=None):
            picked = sb(name, [P, count], dtype, buffer)
            nc.vector.tensor_copy(picked[:], table[:].indirect(offsets[:]))
            return picked

        def project(name, w_dealt, w_scale_dealt, words, scales):
            banks = []
            for t in range(PACK):
                bank = psum.tile([P, S], F32, name=f"{name}_bank{t}", tag=f"{name}{t}")
                nc.tensor.matmul_mx(
                    out=bank[:],
                    lhsT=w_dealt[:, 2 * P * t : 2 * P * (t + 1)].bitcast(FP4X4),
                    lhsT_scale=w_scale_dealt[:, P * t : P * (t + 1)],
                    rhs=words[:].bitcast(FP8X4),
                    rhs_scale=scales[:],
                    start=True,
                    stop=True,
                )
                banks.append(bank)
            return banks

        w1_dealt = deal_weight_words("w1_dealt", w1_raw)
        x_idx_scales = pick("x_idx_scales", x_scale_table, offs_sb, S, U8)
        x_idx_words = pick("x_idx_words", x_table, offs_sb, S, U32)
        w1_scale_dealt = deal_scales("w1_scale_dealt", w1_scale_raw)
        y_banks = project("y", w1_dealt, w1_scale_dealt, x_idx_words, x_idx_scales)
        x_two_scales = pick("x_two_scales", x_scale_table, two_sb, S, U8)
        x_two_words = pick("x_two_words", x_table, two_sb, S, U32)

        dict_scale_picked = pick("dict_scale_picked", dict_scale_table, k1_sb, H, U8)
        dict_dealt = sb("dict_dealt", [P, H], U32)
        dict_scale_dealt = deal_scales("dict_scale_dealt", dict_scale_picked)
        for r in range(1, 4):
            nc.sync.dma_start(
                dict_scale_dealt[r:P:QUADRANT, :].bitcast(I32),
                dict_scale_dealt[BLOCK_PARTITIONS * r : P : QUADRANT, :].bitcast(I32),
            )

        w2_dealt = deal_weight_words("w2_dealt", w2_raw)
        w2_scale_dealt = deal_scales("w2_scale_dealt", w2_scale_raw)
        d_banks = project("d", w2_dealt, w2_scale_dealt, x_two_words, x_two_scales)

        d_n3 = [sb(f"d_n3_{t}", [P, S], F32) for t in range(PACK)]
        term1 = sb("term1", [P, PACK, S], F32)
        term2 = sb("term2", [P, PACK, S], F32)
        halves = [slice(0, S // 2), slice(S // 2, S)]
        diff_n2 = []

        def differences(row_tiles, buffer):
            diffs = sb(f"diffs{row_tiles[0]}", [P, len(row_tiles), 2, S], F32, buffer)
            for i, t in enumerate(row_tiles):
                y = y_win[t][:, :S]
                gs_d = d_win[t][:, :S]
                y_near = sb(f"y_near{t}", [P, 2, S], F32, after_tile_1 if t == 1 else None)
                nc.scalar.activation(y, y_banks[t][:], ACT.Copy)
                nc.scalar.activation(y_near[:, 0, :], y_win[t][:].indirect(n1_sb[:]), ACT.Copy)
                nc.scalar.activation(y_near[:, 1, :], y_win[t][:].indirect(n2_sb[:]), ACT.Copy)
                if t < D_COPIES_ON_VECTOR:
                    nc.vector.tensor_scalar(gs_d, d_banks[t][:], gs_sb[:, t : t + 1], None, ALU.mult)
                else:
                    nc.scalar.activation(gs_d, d_banks[t][:], ACT.Copy, scale=gs_sb[:, t : t + 1])
                nc.vector.tensor_tensor(diffs[:, i, :, :], y_near[:], y.unsqueeze(1).broadcast_to([P, 2, S]), ALU.subtract)
                nc.vector.tensor_tensor(term1[:, t, :], diffs[:, i, 0, :], gs_d, ALU.mult)
                diff_n2.append(diffs[:, i, 1, :])

        differences([0, 1], after_w2)
        dict_picked = pick("dict_picked", dict_table, k1_sb, H, U32, after_tile_1)
        deal(dict_dealt[:], dict_picked[:], 4)
        differences([2, 3], after_tile_1)

        for t in range(PACK):
            for cols in halves if t == PACK - 1 else [slice(0, S)]:
                entries = n3_sb[:, cols.start // LIST_ROWS : cols.stop // LIST_ROWS]
                nc.scalar.activation(d_n3[t][:, cols], d_win[t][:].indirect(entries), ACT.Copy)
                nc.vector.scalar_tensor_tensor(term2[:, t, cols], d_n3[t][:, cols], 0.5, diff_n2[t][:, cols], ALU.mult, ALU.mult)

        h_banks = [psum.tile([P, S], F32, name=f"h_bank{t}", tag=f"y{t}") for t in range(PACK)]
        for u, cols in enumerate(halves):
            z_bf = sb(f"z_bf{u}", [P, S // 2, PACK], BF16)
            nc.vector.tensor_tensor(by_word(z_bf[:]), by_row_tile(term1[:, :, cols]), by_row_tile(term2[:, :, cols]), ALU.add)
            z_words = sb(f"z_words{u}", [P, S // 2], U32)
            z_scales = sb(f"z_scales{u}", [P, S // 2], U8)
            nc.vector.quantize_mx(out=z_words[:].bitcast(FP8X4), scales=z_scales[:], in_=z_bf[:].rearrange("p j t -> p (j t)"))
            for t in range(PACK):
                nc.tensor.matmul_mx(
                    out=h_banks[t][:, cols],
                    lhsT=dict_dealt[:, P * t : P * (t + 1)].bitcast(FP8X4),
                    lhsT_scale=dict_scale_dealt[:, P * t : P * (t + 1)],
                    rhs=z_words[:].bitcast(FP8X4),
                    rhs_scale=z_scales[:],
                    start=True,
                    stop=True,
                )

        def row_tiles_of(name):
            return [sb(f"{name}{t}", [P, S], F32) for t in range(PACK)]

        e_n4, near, total, root, factor = (row_tiles_of(name) for name in ("e_n4_", "near", "total", "root", "factor"))
        result = sb("result", [P, PACK, S], F32)
        for t in range(PACK):
            nc.scalar.activation(e_win[t][:, :S], h_banks[t][:], ACT.Exp, scale=H_TO_EXPONENT)
            nc.scalar.activation(e_n4[t][:], e_win[t][:].indirect(n4_sb[:]), ACT.Copy)
            nc.vector.tensor_tensor(near[t][:], e_win[t][:].indirect(n5_sb[:]), e_n4[t][:], ALU.add)
            nc.vector.tensor_tensor(total[t][:], near[t][:], e_win[t][:, :S], ALU.add)
        for t in range(PACK):
            nc.scalar.activation(root[t][:], total[t][:], ACT.Abs_reciprocal_sqrt, scale=0.5)
        for t in range(SQUARES_ON_VECTOR):
            nc.vector.tensor_tensor(factor[t][:], root[t][:], e_win[t][:, :S], ALU.mult)
        for t in range(SQUARES_ON_VECTOR):
            nc.vector.tensor_tensor(result[:, t, :], factor[t][:], root[t][:], ALU.mult)
        for t in range(SQUARES_ON_VECTOR, PACK):
            nc.scalar.activation(factor[t][:], root[t][:], ACT.Square)
            nc.vector.tensor_tensor(result[:, t, :], factor[t][:], e_win[t][:, :S], ALU.mult)
        out_rows = out_0.rearrange("(p t) j -> p t j", t=PACK)
        for t in range(PACK):
            nc.sync.dma_start(out_rows[:, t, :], result[:, t, :])

        result_bf = sb("result_bf", [P, S, PACK], BF16)
        nc.vector.tensor_copy(by_word(result_bf[:, :CAST_COLUMNS_ON_VECTOR, :]), by_row_tile(result[:, :, :CAST_COLUMNS_ON_VECTOR]))
        nc.scalar.copy(by_word(result_bf[:, CAST_COLUMNS_ON_VECTOR:, :]), by_row_tile(result[:, :, CAST_COLUMNS_ON_VECTOR:]))
        out_words = sb("out_words", [P, S], U32)
        out_scales = sb("out_scales", [P, S], U8)
        nc.vector.quantize_mx(out=out_words[:].bitcast(FP8X4), scales=out_scales[:], in_=result_bf[:].rearrange("p j t -> p (j t)"))
        nc.sync.dma_start(out_1[0].rearrange("p n t -> p (n t)").bitcast(I32), out_words[:].bitcast(I32))
        for q in range(P // QUADRANT):
            queue = nc.scalar if q % 2 == 0 else nc.sync
            queue.dma_start(out_2[0, 4 * q : 4 * q + 4, :].bitcast(I32), out_scales[QUADRANT * q : QUADRANT * q + 4, :].bitcast(I32))
